import numpy as np
import ml_dtypes


def mxq(x, axis, fmt="e4m3"):
    dtype, down = {"e4m3": (ml_dtypes.float8_e4m3fn, 7), "e5m2": (ml_dtypes.float8_e5m2, 14)}[fmt]
    v = np.moveaxis(np.asarray(x, np.float32).astype(ml_dtypes.bfloat16).astype(np.float64), axis, -1)
    blocks = v.reshape(v.shape[:-1] + (-1, 32))
    amax = np.abs(blocks).max(-1, keepdims=True)
    byte = np.maximum(np.where(amax > 0, np.frexp(amax)[1] - 1 + 127, 0) - down, 1)
    scale = np.exp2(byte - 127.0)
    codes = (blocks / scale).astype(np.float32).astype(dtype).astype(np.float64)
    return np.moveaxis((codes * scale).reshape(v.shape), -1, axis)


WIDE = False


def mx_kscale(k):
    if not WIDE:
        return np.ones(k)
    levels = np.array([10, -10, 5, -5, 0])
    if k % 512:
        return np.exp2(np.random.permutation(np.resize(levels, k // 32))).repeat(32)
    a = np.empty((k // 512, 16))
    for p in range(k // 512):
        a[p, :8] = np.random.permutation(np.resize(levels, 8))
        for g in range(8):
            far = levels[np.abs(levels - a[p, g]) >= 10]
            a[p, g + 8] = far[np.random.randint(len(far))]
    return np.exp2(a.ravel()).repeat(32)


def f64(x):
    return np.asarray(x).astype(np.float64)


def striped(idx):
    return np.tile(idx.reshape(-1, 16).T, (8, 1)).astype(np.uint16)


def unstriped(offs):
    return offs[:16].T.reshape(-1).astype(np.int64)


def pack_weight(w):
    k, n = w.shape
    w = f64(np.asarray(w, np.float32).astype(ml_dtypes.bfloat16)).reshape(k // 32, 32, n)
    amax = np.abs(w).max(1)
    byte = np.clip(np.where(amax > 0, np.frexp(amax)[1] - 1 + 127 - 7, 1), 1, 254)
    scaled = (w * np.exp2(127.0 - byte)[:, None, :]).reshape(k, n).astype(np.float32)
    words = np.ascontiguousarray(scaled.reshape(k // 512, 128, 4, n).transpose(0, 1, 3, 2)).astype(ml_dtypes.float8_e4m3fn).view(np.uint8)
    return words, np.ascontiguousarray(byte.astype(np.uint8).reshape(k // 512, 16, n))


def unpack_weight(words, scales):
    g, p, n, _ = words.shape
    vals = np.ascontiguousarray(words).view(ml_dtypes.float8_e4m3fn).astype(np.float64) * np.repeat(np.exp2(scales.astype(np.float64) - 127.0), 8, axis=1)[..., None]
    return vals.transpose(0, 1, 3, 2).reshape(g * 512, n)


K, T, S, D, N = 512, 2048, 512, 4, 256


def setup_inputs():
    n = np.random.standard_normal
    s = mx_kscale(K)[:, None]
    packed_xT = pack_weight(n((K, T)) * s)
    return {
        "x_words": packed_xT[0],
        "x_scales": packed_xT[1],
        "w1": (n((K, N)) / np.sqrt(K) / s).astype(np.float32),
        "w2": (n((K, N)) / np.sqrt(K) / s).astype(np.float32),
        "liq": (np.random.uniform(0.5, 2.0, (N, 1))).astype(np.float32),
        "offs": striped(np.random.permutation(T)[:S]),
    }


def reference(x_words, x_scales, w1, w2, liq, offs):
    xq = unpack_weight(x_words, x_scales)[:, unstriped(offs)]
    yq = mxq(f64(w1), 0, "e4m3").T @ xq
    yb = mxq(f64(w2), 0, "e4m3").T @ xq
    trd = 0.8 * np.tanh(yb)
    qnew = yq + trd
    topb = qnew.reshape(len(qnew), -1, D).max(axis=2)
    exb = np.exp(qnew - np.repeat(topb, D, axis=1))
    costb = topb + np.log(exb.reshape(len(exb), -1, D).sum(axis=2))
    topa = yq.reshape(len(yq), -1, D).max(axis=2)
    exa = np.exp(yq - np.repeat(topa, D, axis=1))
    costa = topa + np.log(exa.reshape(len(exa), -1, D).sum(axis=2))
    return f64(liq) * (costb - costa)

@@ -1,0 +1,125 @@
+from contextlib import ExitStack
+
+import concourse.mybir as mybir
+from concourse.masks import make_identity
+
+K, T, S, D, N = 512, 2048, 512, 4, 256
+FLOPS = 2 * 2 * K * N * S
+
+F32 = mybir.dt.float32
+BF16 = mybir.dt.bfloat16
+I32 = mybir.dt.int32
+U32 = mybir.dt.uint32
+U16 = mybir.dt.uint16
+U8 = mybir.dt.uint8
+FP8X4 = mybir.dt.float8_e4m3fn_x4
+ACT = mybir.ActivationFunctionType
+ALU = mybir.AluOpType
+AXIS = mybir.AxisListType
+
+P = 128
+PACK = 4
+V = S // D
+HALVES = N // P
+
+
+def tile_picked_ylmsr_cost_p_kernel(tc, x_words, x_scales, w1, w2, liq, offs, out):
+    nc = tc.nc
+    with ExitStack() as ctx:
+        sb = ctx.enter_context(tc.tile_pool(name="sb", bufs=1))
+        ps = ctx.enter_context(tc.psum_pool(name="ps", bufs=1))
+
+        offsets = sb.tile([P, S // 16], U16, name="offsets")
+        table_scales = sb.tile([P, T], U8, name="table_scales", align_bytes=64)
+        table_words = sb.tile([P, T], I32, name="table_words", align_bytes=64)
+        raw = [sb.tile([P, PACK, N], F32, name="raw%d" % i, align_bytes=64) for i in range(2)]
+        liq_sb = sb.tile([P, HALVES], F32, name="liq_sb")
+
+        nc.sync.dma_start(offsets[:], offs)
+        nc.vector.memset(table_scales[:].bitcast(I32), 0)
+        scale_rows = x_scales[0].bitcast(I32)
+        for q in range(4):
+            nc.scalar.dma_start(table_scales[32 * q : 32 * q + 4, :].bitcast(I32), scale_rows[4 * q : 4 * (q + 1), :])
+        nc.sync.dma_start(table_words[:], x_words[0].rearrange("p c r -> p (c r)").bitcast(I32))
+        nc.sync.dma_start(raw[1][:], w2.rearrange("(p j) n -> p j n", j=PACK))
+        nc.sync.dma_start(raw[0][:], w1.rearrange("(p j) n -> p j n", j=PACK))
+        with nc.allow_non_contiguous_dma(reason="one liquidity a partition"):
+            nc.sync.dma_start(liq_sb[:], liq.rearrange("(h p) o -> p (h o)", p=P))
+
+        ident = sb.tile([P, P], F32, name="ident")
+        make_identity(nc, ident[:])
+
+        picked_scales = sb.tile([P, S], U8, name="picked_scales", align_bytes=64)
+        nc.vector.tensor_copy(picked_scales[:], table_scales[:].indirect(offsets[:]))
+        x_scale = sb.tile([P, D, V], U8, name="x_scale", align_bytes=64)
+        nc.vector.tensor_copy(x_scale[:], picked_scales[:].rearrange("p (v d) -> p d v", d=D))
+        x_code = sb.tile([P, D, V], U32, name="x_code", align_bytes=64)
+        nc.vector.tensor_copy(
+            x_code[:].rearrange("p d v -> p v d"), table_words[:].bitcast(U32).indirect(offsets[:])
+        )
+
+        def product(i, h, cast):
+            name = "%d%d" % (i, h)
+            grouped = sb.tile([P, P, PACK], BF16, name="grouped" + name, align_bytes=64)
+            cast(grouped[:], raw[i][:, :, P * h : P * (h + 1)].rearrange("p j n -> p n j"))
+            codes = sb.tile([P, P], U32, name="codes" + name, align_bytes=64)
+            scales = sb.tile([P, P], U8, name="scales" + name, align_bytes=64)
+            nc.vector.quantize_mx(
+                out=codes[:].bitcast(FP8X4), scales=scales[:], in_=grouped[:].rearrange("p n j -> p (n j)")
+            )
+            y = ps.tile([P, D, P], F32, name="y" + name)
+            for d in range(D):
+                nc.tensor.matmul_mx(
+                    out=y[:, d, :],
+                    lhsT=x_code[:, d, :].bitcast(FP8X4),
+                    lhsT_scale=x_scale[:, d, :],
+                    rhs=codes[:].bitcast(FP8X4),
+                    rhs_scale=scales[:],
+                    start=True,
+                    stop=True,
+                )
+            return y
+
+        def sum_over_outcomes(total, terms):
+            for d in range(D):
+                nc.tensor.matmul(
+                    total, lhsT=terms[:, d, :], rhs=ident[:], is_transpose=True, start=(d == 0), stop=(d == D - 1)
+                )
+
+        yb = [product(1, h, nc.scalar.copy) for h in range(HALVES)]
+        yq = [product(0, 0, nc.vector.tensor_copy), product(0, 1, nc.scalar.copy)]
+
+        sum_a = ps.tile([P, HALVES, V], F32, name="sum_a")
+        sum_b = [ps.tile([P, V], F32, name="sum_b%d" % h) for h in range(HALVES)]
+        growth, ea = [], []
+        for h in range(HALVES):
+            trade = sb.tile([P, D, P], F32, name="trade%d" % h)
+            nc.scalar.activation(trade[:], yb[h][:], ACT.Tanh)
+            top = sb.tile([P, P], F32, name="top%d" % h)
+            nc.vector.tensor_reduce(top[:], yq[h][:].rearrange("p d m -> p m d"), AXIS.X, ALU.max)
+            shifted = sb.tile([P, D, P], F32, name="shifted%d" % h)
+            nc.vector.tensor_tensor(shifted[:], yq[h][:], top[:].unsqueeze(1).to_broadcast([P, D, P]), ALU.subtract)
+            e = sb.tile([P, D, P], F32, name="ea%d" % h)
+            nc.scalar.activation(e[:], shifted[:], ACT.Exp)
+            ea.append(e)
+            g = sb.tile([P, D, P], F32, name="growth%d" % h)
+            nc.scalar.activation(g[:], trade[:], ACT.Exp, scale=0.8)
+            growth.append(g)
+        for h in range(HALVES):
+            sum_over_outcomes(sum_a[:, h, :], ea[h])
+            eb = sb.tile([P, D, P], F32, name="eb%d" % h)
+            nc.vector.tensor_tensor(eb[:], ea[h][:], growth[h][:], ALU.mult)
+            sum_over_outcomes(sum_b[h][:], eb)
+
+        log_a = sb.tile([P, HALVES, V], F32, name="log_a")
+        nc.scalar.activation(log_a[:], sum_a[:], ACT.Ln)
+        for h in range(HALVES):
+            cost_a = sb.tile([P, V], F32, name="cost_a%d" % h)
+            nc.vector.tensor_scalar_mul(cost_a[:], log_a[:, h, :], liq_sb[:, h : h + 1])
+            log_b = sb.tile([P, V], F32, name="log_b%d" % h)
+            nc.scalar.activation(log_b[:], sum_b[h][:], ACT.Ln)
+            result = sb.tile([P, V], F32, name="result%d" % h)
+            nc.vector.scalar_tensor_tensor(
+                result[:], log_b[:], liq_sb[:, h : h + 1], cost_a[:], ALU.mult, ALU.subtract
+            )
+            nc.sync.dma_start(out[P * h : P * (h + 1), :], result[:])

@@ -31,16 +31,19 @@ def tile_picked_ylmsr_cost_p_kernel(tc, x_words, x_scales, w1, w2, liq, offs, ou
 
         offsets = sb.tile([P, S // 16], U16, name="offsets")
         table_scales = sb.tile([P, T], U8, name="table_scales", align_bytes=64)
-        table_words = sb.tile([P, T], I32, name="table_words", align_bytes=64)
-        raw = [sb.tile([P, PACK, N], F32, name="raw%d" % i, align_bytes=64) for i in range(2)]
+        table_words = sb.tile([P, T], I32, name="table_words", tag="words", align_bytes=64)
+        raw = [sb.tile([P, PACK, N], F32, name="raw%d" % i, tag="raw%d" % i, align_bytes=64) for i in range(2)]
         liq_sb = sb.tile([P, HALVES], F32, name="liq_sb")
 
         nc.sync.dma_start(offsets[:], offs)
+        word_rows = x_words[0].rearrange("p c r -> p (c r)").bitcast(I32)
+        nc.sync.dma_start(table_words[:, :384], word_rows[:, :384])
         nc.vector.memset(table_scales[:].bitcast(I32), 0)
         scale_rows = x_scales[0].bitcast(I32)
         for q in range(4):
-            nc.scalar.dma_start(table_scales[32 * q : 32 * q + 4, :].bitcast(I32), scale_rows[4 * q : 4 * (q + 1), :])
-        nc.sync.dma_start(table_words[:], x_words[0].rearrange("p c r -> p (c r)").bitcast(I32))
+            queue = nc.scalar if q % 2 else nc.sync
+            queue.dma_start(table_scales[32 * q : 32 * q + 4, :].bitcast(I32), scale_rows[4 * q : 4 * (q + 1), :])
+        nc.sync.dma_start(table_words[:, 384:], word_rows[:, 384:])
         nc.sync.dma_start(raw[1][:], w2.rearrange("(p j) n -> p j n", j=PACK))
         nc.sync.dma_start(raw[0][:], w1.rearrange("(p j) n -> p j n", j=PACK))
         with nc.allow_non_contiguous_dma(reason="one liquidity a partition"):
@@ -49,25 +52,29 @@ def tile_picked_ylmsr_cost_p_kernel(tc, x_words, x_scales, w1, w2, liq, offs, ou
         ident = sb.tile([P, P], F32, name="ident")
         make_identity(nc, ident[:])
 
-        picked_scales = sb.tile([P, S], U8, name="picked_scales", align_bytes=64)
+        picked_scales = sb.tile([P, S], U8, name="picked_scales", tag="picked", align_bytes=64)
         nc.vector.tensor_copy(picked_scales[:], table_scales[:].indirect(offsets[:]))
         x_scale = sb.tile([P, D, V], U8, name="x_scale", align_bytes=64)
         nc.vector.tensor_copy(x_scale[:], picked_scales[:].rearrange("p (v d) -> p d v", d=D))
-        x_code = sb.tile([P, D, V], U32, name="x_code", align_bytes=64)
+        x_code = sb.tile([P, D, V], U32, name="x_code", tag="picked", align_bytes=64)
         nc.vector.tensor_copy(
             x_code[:].rearrange("p d v -> p v d"), table_words[:].bitcast(U32).indirect(offsets[:])
         )
 
-        def product(i, h, cast):
+        def quantise(i, h, cast, grouped_tag, codes_tag):
             name = "%d%d" % (i, h)
-            grouped = sb.tile([P, P, PACK], BF16, name="grouped" + name, align_bytes=64)
+            grouped = sb.tile([P, P, PACK], BF16, name="grouped" + name, tag=grouped_tag, align_bytes=64)
             cast(grouped[:], raw[i][:, :, P * h : P * (h + 1)].rearrange("p j n -> p n j"))
-            codes = sb.tile([P, P], U32, name="codes" + name, align_bytes=64)
+            codes = sb.tile([P, P], U32, name="codes" + name, tag=codes_tag, align_bytes=64)
             scales = sb.tile([P, P], U8, name="scales" + name, align_bytes=64)
             nc.vector.quantize_mx(
                 out=codes[:].bitcast(FP8X4), scales=scales[:], in_=grouped[:].rearrange("p n j -> p (n j)")
             )
-            y = ps.tile([P, D, P], F32, name="y" + name)
+            return codes, scales
+
+        def product(name, weights):
+            codes, scales = weights
+            y = ps.tile([P, D, P], F32, name=name)
             for d in range(D):
                 nc.tensor.matmul_mx(
                     out=y[:, d, :],
@@ -86,25 +93,33 @@ def tile_picked_ylmsr_cost_p_kernel(tc, x_words, x_scales, w1, w2, liq, offs, ou
                     total, lhsT=terms[:, d, :], rhs=ident[:], is_transpose=True, start=(d == 0), stop=(d == D - 1)
                 )
 
-        yb = [product(1, h, nc.scalar.copy) for h in range(HALVES)]
-        yq = [product(0, 0, nc.vector.tensor_copy), product(0, 1, nc.scalar.copy)]
+        yb = [product("yb0", quantise(1, 0, nc.scalar.copy, "g10", "words"))]
+        first = quantise(0, 0, nc.vector.tensor_copy, "g10", "c00")
+        yb.append(product("yb1", quantise(1, 1, nc.scalar.copy, "g11", "c11")))
+        yq = [product("yq0", first), product("yq1", quantise(0, 1, nc.scalar.copy, "g01", "c01"))]
 
         sum_a = ps.tile([P, HALVES, V], F32, name="sum_a")
         sum_b = [ps.tile([P, V], F32, name="sum_b%d" % h) for h in range(HALVES)]
-        growth, ea = [], []
+        growth, ea, top = [], [], []
         for h in range(HALVES):
-            trade = sb.tile([P, D, P], F32, name="trade%d" % h)
+            trade = sb.tile([P, D, P], F32, name="trade%d" % h, tag=("raw0", "g01")[h], align_bytes=64)
             nc.scalar.activation(trade[:], yb[h][:], ACT.Tanh)
-            top = sb.tile([P, P], F32, name="top%d" % h)
-            nc.vector.tensor_reduce(top[:], yq[h][:].rearrange("p d m -> p m d"), AXIS.X, ALU.max)
-            shifted = sb.tile([P, D, P], F32, name="shifted%d" % h)
-            nc.vector.tensor_tensor(shifted[:], yq[h][:], top[:].unsqueeze(1).to_broadcast([P, D, P]), ALU.subtract)
-            e = sb.tile([P, D, P], F32, name="ea%d" % h)
-            nc.scalar.activation(e[:], shifted[:], ACT.Exp)
-            ea.append(e)
             g = sb.tile([P, D, P], F32, name="growth%d" % h)
             nc.scalar.activation(g[:], trade[:], ACT.Exp, scale=0.8)
             growth.append(g)
+            t = sb.tile([P, P], F32, name="top%d" % h)
+            nc.vector.tensor_reduce(t[:], yq[h][:].rearrange("p d m -> p m d"), AXIS.X, ALU.max)
+            top.append(t)
+        for h in range(HALVES):
+            shifted = sb.tile([P, D, P], F32, name="shifted%d" % h)
+            e = sb.tile([P, D, P], F32, name="ea%d" % h)
+            for d0 in range(0, D, 2):
+                part = slice(d0, d0 + 2)
+                nc.vector.tensor_tensor(
+                    shifted[:, part, :], yq[h][:, part, :], top[h][:].unsqueeze(1).to_broadcast([P, 2, P]), ALU.subtract
+                )
+                nc.scalar.activation(e[:, part, :], shifted[:, part, :], ACT.Exp)
+            ea.append(e)
         for h in range(HALVES):
             sum_over_outcomes(sum_a[:, h, :], ea[h])
             eb = sb.tile([P, D, P], F32, name="eb%d" % h)

@@ -32,31 +32,36 @@ def tile_picked_ylmsr_cost_p_kernel(tc, x_words, x_scales, w1, w2, liq, offs, ou
         offsets = sb.tile([P, S // 16], U16, name="offsets")
         table_scales = sb.tile([P, T], U8, name="table_scales", align_bytes=64)
         table_words = sb.tile([P, T], I32, name="table_words", tag="words", align_bytes=64)
-        raw = [sb.tile([P, PACK, N], F32, name="raw%d" % i, tag="raw%d" % i, align_bytes=64) for i in range(2)]
+        raw = {
+            (i, h): sb.tile([P, PACK, P], F32, name="raw%d%d" % (i, h), tag="raw%d%d" % (i, h), align_bytes=64)
+            for i in range(2)
+            for h in range(HALVES)
+        }
         liq_sb = sb.tile([P, HALVES], F32, name="liq_sb")
 
-        nc.sync.dma_start(offsets[:], offs)
         word_rows = x_words[0].rearrange("p c r -> p (c r)").bitcast(I32)
         nc.sync.dma_start(table_words[:, :384], word_rows[:, :384])
+        nc.sync.dma_start(offsets[:], offs)
         nc.vector.memset(table_scales[:].bitcast(I32), 0)
         scale_rows = x_scales[0].bitcast(I32)
         for q in range(4):
             queue = nc.scalar if q % 2 else nc.sync
             queue.dma_start(table_scales[32 * q : 32 * q + 4, :].bitcast(I32), scale_rows[4 * q : 4 * (q + 1), :])
         nc.sync.dma_start(table_words[:, 384:], word_rows[:, 384:])
-        nc.sync.dma_start(raw[1][:], w2.rearrange("(p j) n -> p j n", j=PACK))
-        nc.sync.dma_start(raw[0][:], w1.rearrange("(p j) n -> p j n", j=PACK))
+        for h in range(HALVES):
+            for i, w in ((1, w2), (0, w1)):
+                nc.sync.dma_start(raw[i, h][:], w.rearrange("(p j) n -> p j n", j=PACK)[:, :, P * h : P * (h + 1)])
         with nc.allow_non_contiguous_dma(reason="one liquidity a partition"):
             nc.sync.dma_start(liq_sb[:], liq.rearrange("(h p) o -> p (h o)", p=P))
 
         ident = sb.tile([P, P], F32, name="ident")
         make_identity(nc, ident[:])
 
-        picked_scales = sb.tile([P, S], U8, name="picked_scales", tag="picked", align_bytes=64)
+        picked_scales = sb.tile([P, S], U8, name="picked_scales", align_bytes=64)
         nc.vector.tensor_copy(picked_scales[:], table_scales[:].indirect(offsets[:]))
         x_scale = sb.tile([P, D, V], U8, name="x_scale", align_bytes=64)
         nc.vector.tensor_copy(x_scale[:], picked_scales[:].rearrange("p (v d) -> p d v", d=D))
-        x_code = sb.tile([P, D, V], U32, name="x_code", tag="picked", align_bytes=64)
+        x_code = sb.tile([P, D, V], U32, name="x_code", align_bytes=64)
         nc.vector.tensor_copy(
             x_code[:].rearrange("p d v -> p v d"), table_words[:].bitcast(U32).indirect(offsets[:])
         )
@@ -64,7 +69,10 @@ def tile_picked_ylmsr_cost_p_kernel(tc, x_words, x_scales, w1, w2, liq, offs, ou
         def quantise(i, h, cast, grouped_tag, codes_tag):
             name = "%d%d" % (i, h)
             grouped = sb.tile([P, P, PACK], BF16, name="grouped" + name, tag=grouped_tag, align_bytes=64)
-            cast(grouped[:], raw[i][:, :, P * h : P * (h + 1)].rearrange("p j n -> p n j"))
+            cast(
+                grouped[:].rearrange("p (c i) j -> p c j i", i=4),
+                raw[i, h][:].rearrange("p j (c i) -> p c j i", i=4),
+            )
             codes = sb.tile([P, P], U32, name="codes" + name, tag=codes_tag, align_bytes=64)
             scales = sb.tile([P, P], U8, name="scales" + name, align_bytes=64)
             nc.vector.quantize_mx(
@@ -93,32 +101,35 @@ def tile_picked_ylmsr_cost_p_kernel(tc, x_words, x_scales, w1, w2, liq, offs, ou
                     total, lhsT=terms[:, d, :], rhs=ident[:], is_transpose=True, start=(d == 0), stop=(d == D - 1)
                 )
 
-        yb = [product("yb0", quantise(1, 0, nc.scalar.copy, "g10", "words"))]
-        first = quantise(0, 0, nc.vector.tensor_copy, "g10", "c00")
-        yb.append(product("yb1", quantise(1, 1, nc.scalar.copy, "g11", "c11")))
-        yq = [product("yq0", first), product("yq1", quantise(0, 1, nc.scalar.copy, "g01", "c01"))]
+        yb, yq = [], []
+        for h, cast in enumerate((nc.scalar.copy, nc.vector.tensor_copy)):
+            yb.append(product("yb%d" % h, quantise(1, h, cast, "g1", ("words", "c11")[h])))
+            yq.append(product("yq%d" % h, quantise(0, h, cast, "g0", "c0%d" % h)))
 
         sum_a = ps.tile([P, HALVES, V], F32, name="sum_a")
         sum_b = [ps.tile([P, V], F32, name="sum_b%d" % h) for h in range(HALVES)]
+        parts = [slice(m0, m0 + P // 2) for m0 in range(0, P, P // 2)]
         growth, ea, top = [], [], []
         for h in range(HALVES):
-            trade = sb.tile([P, D, P], F32, name="trade%d" % h, tag=("raw0", "g01")[h], align_bytes=64)
+            trade = sb.tile([P, D, P], F32, name="trade%d" % h, tag="raw%d0" % h, align_bytes=64)
             nc.scalar.activation(trade[:], yb[h][:], ACT.Tanh)
+            t = sb.tile([P, P], F32, name="top%d" % h, tag=("raw01", "top1")[h], align_bytes=64)
+            for part in parts:
+                nc.vector.tensor_reduce(t[:, part], yq[h][:, :, part].rearrange("p d m -> p m d"), AXIS.X, ALU.max)
+            top.append(t)
+            shifted = sb.tile([P, D, P], F32, name="shifted%d" % h)
+            e = sb.tile([P, D, P], F32, name="ea%d" % h)
             g = sb.tile([P, D, P], F32, name="growth%d" % h)
             nc.scalar.activation(g[:], trade[:], ACT.Exp, scale=0.8)
             growth.append(g)
-            t = sb.tile([P, P], F32, name="top%d" % h)
-            nc.vector.tensor_reduce(t[:], yq[h][:].rearrange("p d m -> p m d"), AXIS.X, ALU.max)
-            top.append(t)
-        for h in range(HALVES):
-            shifted = sb.tile([P, D, P], F32, name="shifted%d" % h)
-            e = sb.tile([P, D, P], F32, name="ea%d" % h)
-            for d0 in range(0, D, 2):
-                part = slice(d0, d0 + 2)
+            for part in parts:
                 nc.vector.tensor_tensor(
-                    shifted[:, part, :], yq[h][:, part, :], top[h][:].unsqueeze(1).to_broadcast([P, 2, P]), ALU.subtract
+                    shifted[:, :, part],
+                    yq[h][:, :, part],
+                    t[:, part].unsqueeze(1).to_broadcast([P, D, P // 2]),
+                    ALU.subtract,
                 )
-                nc.scalar.activation(e[:, part, :], shifted[:, part, :], ACT.Exp)
+                nc.scalar.activation(e[:, :, part], shifted[:, :, part], ACT.Exp)
             ea.append(e)
         for h in range(HALVES):
             sum_over_outcomes(sum_a[:, h, :], ea[h])
@@ -128,13 +139,14 @@ def tile_picked_ylmsr_cost_p_kernel(tc, x_words, x_scales, w1, w2, liq, offs, ou
 
         log_a = sb.tile([P, HALVES, V], F32, name="log_a")
         nc.scalar.activation(log_a[:], sum_a[:], ACT.Ln)
+        cost_a = sb.tile([P, HALVES, V], F32, name="cost_a")
         for h in range(HALVES):
-            cost_a = sb.tile([P, V], F32, name="cost_a%d" % h)
-            nc.vector.tensor_scalar_mul(cost_a[:], log_a[:, h, :], liq_sb[:, h : h + 1])
+            nc.vector.tensor_scalar_mul(cost_a[:, h, :], log_a[:, h, :], liq_sb[:, h : h + 1])
+        for h in range(HALVES):
             log_b = sb.tile([P, V], F32, name="log_b%d" % h)
             nc.scalar.activation(log_b[:], sum_b[h][:], ACT.Ln)
             result = sb.tile([P, V], F32, name="result%d" % h)
             nc.vector.scalar_tensor_tensor(
-                result[:], log_b[:], liq_sb[:, h : h + 1], cost_a[:], ALU.mult, ALU.subtract
+                result[:], log_b[:], liq_sb[:, h : h + 1], cost_a[:, h, :], ALU.mult, ALU.subtract
             )
             nc.sync.dma_start(out[P * h : P * (h + 1), :], result[:])

@@ -21,6 +21,11 @@ P = 128
 PACK = 4
 V = S // D
 HALVES = N // P
+PART = P // 2
+QUADRANT = 32
+LINE = 4
+WORDS_AHEAD = 384
+TRADE_LIMIT = 0.8
 
 
 def tile_picked_ylmsr_cost_p_kernel(tc, x_words, x_scales, w1, w2, liq, offs, out):
@@ -29,29 +34,33 @@ def tile_picked_ylmsr_cost_p_kernel(tc, x_words, x_scales, w1, w2, liq, offs, ou
         sb = ctx.enter_context(tc.tile_pool(name="sb", bufs=1))
         ps = ctx.enter_context(tc.psum_pool(name="ps", bufs=1))
 
+
         offsets = sb.tile([P, S // 16], U16, name="offsets")
         table_scales = sb.tile([P, T], U8, name="table_scales", align_bytes=64)
         table_words = sb.tile([P, T], I32, name="table_words", tag="words", align_bytes=64)
         raw = {
-            (i, h): sb.tile([P, PACK, P], F32, name="raw%d%d" % (i, h), tag="raw%d%d" % (i, h), align_bytes=64)
-            for i in range(2)
+            (w, h): sb.tile([P, PACK, P], F32, name="raw_%s_%d" % (w, h), tag="raw_%s_%d" % (w, h), align_bytes=64)
+            for w in ("w1", "w2")
             for h in range(HALVES)
         }
         liq_sb = sb.tile([P, HALVES], F32, name="liq_sb")
 
         word_rows = x_words[0].rearrange("p c r -> p (c r)").bitcast(I32)
-        nc.sync.dma_start(table_words[:, :384], word_rows[:, :384])
+        nc.sync.dma_start(table_words[:, :WORDS_AHEAD], word_rows[:, :WORDS_AHEAD])
         nc.sync.dma_start(offsets[:], offs)
         nc.vector.memset(table_scales[:].bitcast(I32), 0)
         scale_rows = x_scales[0].bitcast(I32)
-        for q in range(4):
+        for q in range(P // QUADRANT):
             queue = nc.scalar if q % 2 else nc.sync
-            queue.dma_start(table_scales[32 * q : 32 * q + 4, :].bitcast(I32), scale_rows[4 * q : 4 * (q + 1), :])
-        nc.sync.dma_start(table_words[:, 384:], word_rows[:, 384:])
+            queue.dma_start(
+                table_scales[QUADRANT * q : QUADRANT * q + 4, :].bitcast(I32), scale_rows[4 * q : 4 * (q + 1), :]
+            )
+        nc.sync.dma_start(table_words[:, WORDS_AHEAD:], word_rows[:, WORDS_AHEAD:])
         for h in range(HALVES):
-            for i, w in ((1, w2), (0, w1)):
-                nc.sync.dma_start(raw[i, h][:], w.rearrange("(p j) n -> p j n", j=PACK)[:, :, P * h : P * (h + 1)])
-        with nc.allow_non_contiguous_dma(reason="one liquidity a partition"):
+            for w, weight in (("w2", w2), ("w1", w1)):
+                rows = weight.rearrange("(p j) n -> p j n", j=PACK)
+                nc.sync.dma_start(raw[w, h][:], rows[:, :, P * h : P * (h + 1)])
+        with nc.allow_non_contiguous_dma(reason="one liquidity a partition and half"):
             nc.sync.dma_start(liq_sb[:], liq.rearrange("(h p) o -> p (h o)", p=P))
 
         ident = sb.tile([P, P], F32, name="ident")
@@ -66,26 +75,26 @@ def tile_picked_ylmsr_cost_p_kernel(tc, x_words, x_scales, w1, w2, liq, offs, ou
             x_code[:].rearrange("p d v -> p v d"), table_words[:].bitcast(U32).indirect(offsets[:])
         )
 
-        def quantise(i, h, cast, grouped_tag, codes_tag):
-            name = "%d%d" % (i, h)
-            grouped = sb.tile([P, P, PACK], BF16, name="grouped" + name, tag=grouped_tag, align_bytes=64)
+        def quantise(w, h, cast, codes_tag):
+            name = "%s_%d" % (w, h)
+            grouped = sb.tile([P, P, PACK], BF16, name="grouped_" + name, tag="grouped_" + w, align_bytes=64)
             cast(
-                grouped[:].rearrange("p (c i) j -> p c j i", i=4),
-                raw[i, h][:].rearrange("p j (c i) -> p c j i", i=4),
+                grouped[:].rearrange("p (c i) j -> p c j i", i=LINE),
+                raw[w, h][:].rearrange("p j (c i) -> p c j i", i=LINE),
             )
-            codes = sb.tile([P, P], U32, name="codes" + name, tag=codes_tag, align_bytes=64)
-            scales = sb.tile([P, P], U8, name="scales" + name, align_bytes=64)
+            codes = sb.tile([P, P], U32, name="codes_" + name, tag=codes_tag, align_bytes=64)
+            scales = sb.tile([P, P], U8, name="scales_" + name, align_bytes=64)
             nc.vector.quantize_mx(
                 out=codes[:].bitcast(FP8X4), scales=scales[:], in_=grouped[:].rearrange("p n j -> p (n j)")
             )
             return codes, scales
 
-        def product(name, weights):
-            codes, scales = weights
-            y = ps.tile([P, D, P], F32, name=name)
-            for d in range(D):
+        def product(name, quantised, planes):
+            codes, scales = quantised
+            y = ps.tile([P, len(planes), P], F32, name=name)
+            for d in planes:
                 nc.tensor.matmul_mx(
-                    out=y[:, d, :],
+                    out=y[:, d - planes.start, :],
                     lhsT=x_code[:, d, :].bitcast(FP8X4),
                     lhsT_scale=x_scale[:, d, :],
                     rhs=codes[:].bitcast(FP8X4),
@@ -101,36 +110,48 @@ def tile_picked_ylmsr_cost_p_kernel(tc, x_words, x_scales, w1, w2, liq, offs, ou
                     total, lhsT=terms[:, d, :], rhs=ident[:], is_transpose=True, start=(d == 0), stop=(d == D - 1)
                 )
 
+        casts = (nc.scalar.copy, nc.vector.tensor_copy)
+        w2_codes_tags = ("words", "codes_w2_1")
+        yb_banks = ((range(0, D // 2), range(D // 2, D)), (range(D),))
         yb, yq = [], []
-        for h, cast in enumerate((nc.scalar.copy, nc.vector.tensor_copy)):
-            yb.append(product("yb%d" % h, quantise(1, h, cast, "g1", ("words", "c11")[h])))
-            yq.append(product("yq%d" % h, quantise(0, h, cast, "g0", "c0%d" % h)))
+        for h in range(HALVES):
+            w2_mx = quantise("w2", h, casts[h], w2_codes_tags[h])
+            yb.append([product("yb%d_%d" % (h, planes.start), w2_mx, planes) for planes in yb_banks[h]])
+            yq.append(product("yq%d" % h, quantise("w1", h, casts[h], "codes_w1_%d" % h), range(D)))
 
         sum_a = ps.tile([P, HALVES, V], F32, name="sum_a")
         sum_b = [ps.tile([P, V], F32, name="sum_b%d" % h) for h in range(HALVES)]
-        parts = [slice(m0, m0 + P // 2) for m0 in range(0, P, P // 2)]
-        growth, ea, top = [], [], []
+        trade_tags = ("raw_w1_0", "raw_w2_0")
+        top_tags = ("raw_w1_1", "top1")
+        growth_tags = ("growth0", "shifted0_0")
+        parts = [slice(m0, m0 + PART) for m0 in range(0, P, PART)]
+        growth, ea = [], []
         for h in range(HALVES):
-            trade = sb.tile([P, D, P], F32, name="trade%d" % h, tag="raw%d0" % h, align_bytes=64)
-            nc.scalar.activation(trade[:], yb[h][:], ACT.Tanh)
-            t = sb.tile([P, P], F32, name="top%d" % h, tag=("raw01", "top1")[h], align_bytes=64)
+            trade = sb.tile([P, D, P], F32, name="trade%d" % h, tag=trade_tags[h], align_bytes=64)
+            for planes, y in zip(yb_banks[h], yb[h]):
+                nc.scalar.activation(trade[:, planes.start : planes.stop, :], y[:], ACT.Tanh)
+            top = sb.tile([P, P], F32, name="top%d" % h, tag=top_tags[h], align_bytes=64)
             for part in parts:
-                nc.vector.tensor_reduce(t[:, part], yq[h][:, :, part].rearrange("p d m -> p m d"), AXIS.X, ALU.max)
-            top.append(t)
-            shifted = sb.tile([P, D, P], F32, name="shifted%d" % h)
-            e = sb.tile([P, D, P], F32, name="ea%d" % h)
-            g = sb.tile([P, D, P], F32, name="growth%d" % h)
-            nc.scalar.activation(g[:], trade[:], ACT.Exp, scale=0.8)
-            growth.append(g)
+                nc.vector.tensor_reduce(top[:, part], yq[h][:, :, part].rearrange("p d m -> p m d"), AXIS.X, ALU.max)
+            ea.append(sb.tile([P, D, P], F32, name="ea%d" % h))
+            growth.append(sb.tile([P, D, P], F32, name="growth%d" % h, tag=growth_tags[h]))
+            for planes in yb_banks[h]:
+                nc.scalar.activation(
+                    growth[h][:, planes.start : planes.stop, :],
+                    trade[:, planes.start : planes.stop, :],
+                    ACT.Exp,
+                    scale=TRADE_LIMIT,
+                )
             for part in parts:
+                name = "shifted%d_%d" % (h, part.start)
+                shifted = sb.tile([P, D, PART], F32, name=name, tag=name)
                 nc.vector.tensor_tensor(
-                    shifted[:, :, part],
+                    shifted[:],
                     yq[h][:, :, part],
-                    t[:, part].unsqueeze(1).to_broadcast([P, D, P // 2]),
+                    top[:, part].unsqueeze(1).to_broadcast([P, D, PART]),
                     ALU.subtract,
                 )
-                nc.scalar.activation(e[:, :, part], shifted[:, :, part], ACT.Exp)
-            ea.append(e)
+                nc.scalar.activation(ea[h][:, :, part], shifted[:], ACT.Exp)
         for h in range(HALVES):
             sum_over_outcomes(sum_a[:, h, :], ea[h])
             eb = sb.tile([P, D, P], F32, name="eb%d" % h)
@@ -138,9 +159,9 @@ def tile_picked_ylmsr_cost_p_kernel(tc, x_words, x_scales, w1, w2, liq, offs, ou
             sum_over_outcomes(sum_b[h][:], eb)
 
         log_a = sb.tile([P, HALVES, V], F32, name="log_a")
-        nc.scalar.activation(log_a[:], sum_a[:], ACT.Ln)
         cost_a = sb.tile([P, HALVES, V], F32, name="cost_a")
         for h in range(HALVES):
+            nc.scalar.activation(log_a[:, h, :], sum_a[:, h, :], ACT.Ln)
             nc.vector.tensor_scalar_mul(cost_a[:, h, :], log_a[:, h, :], liq_sb[:, h : h + 1])
         for h in range(HALVES):
             log_b = sb.tile([P, V], F32, name="log_b%d" % h)

from contextlib import ExitStack

import concourse.mybir as mybir
from concourse.masks import make_identity

K, T, S, D, N = 512, 2048, 512, 4, 256
FLOPS = 2 * 2 * K * N * S

F32 = mybir.dt.float32
BF16 = mybir.dt.bfloat16
I32 = mybir.dt.int32
U32 = mybir.dt.uint32
U16 = mybir.dt.uint16
U8 = mybir.dt.uint8
FP8X4 = mybir.dt.float8_e4m3fn_x4
ACT = mybir.ActivationFunctionType
ALU = mybir.AluOpType
AXIS = mybir.AxisListType

P = 128
PACK = 4
V = S // D
HALVES = N // P
PART = P // 2
QUADRANT = 32
LINE = 4
WORDS_AHEAD = 384
TRADE_LIMIT = 0.8


def tile_picked_ylmsr_cost_p_kernel(tc, x_words, x_scales, w1, w2, liq, offs, out):
    nc = tc.nc
    with ExitStack() as ctx:
        sb = ctx.enter_context(tc.tile_pool(name="sb", bufs=1))
        ps = ctx.enter_context(tc.psum_pool(name="ps", bufs=1))


        offsets = sb.tile([P, S // 16], U16, name="offsets")
        table_scales = sb.tile([P, T], U8, name="table_scales", align_bytes=64)
        table_words = sb.tile([P, T], I32, name="table_words", tag="words", align_bytes=64)
        raw = {
            (w, h): sb.tile([P, PACK, P], F32, name="raw_%s_%d" % (w, h), tag="raw_%s_%d" % (w, h), align_bytes=64)
            for w in ("w1", "w2")
            for h in range(HALVES)
        }
        liq_sb = sb.tile([P, HALVES], F32, name="liq_sb")

        word_rows = x_words[0].rearrange("p c r -> p (c r)").bitcast(I32)
        nc.sync.dma_start(table_words[:, :WORDS_AHEAD], word_rows[:, :WORDS_AHEAD])
        nc.sync.dma_start(offsets[:], offs)
        nc.vector.memset(table_scales[:].bitcast(I32), 0)
        scale_rows = x_scales[0].bitcast(I32)
        for q in range(P // QUADRANT):
            queue = nc.scalar if q % 2 else nc.sync
            queue.dma_start(
                table_scales[QUADRANT * q : QUADRANT * q + 4, :].bitcast(I32), scale_rows[4 * q : 4 * (q + 1), :]
            )
        nc.sync.dma_start(table_words[:, WORDS_AHEAD:], word_rows[:, WORDS_AHEAD:])
        for h in range(HALVES):
            for w, weight in (("w2", w2), ("w1", w1)):
                rows = weight.rearrange("(p j) n -> p j n", j=PACK)
                nc.sync.dma_start(raw[w, h][:], rows[:, :, P * h : P * (h + 1)])
        with nc.allow_non_contiguous_dma(reason="one liquidity a partition and half"):
            nc.sync.dma_start(liq_sb[:], liq.rearrange("(h p) o -> p (h o)", p=P))

        ident = sb.tile([P, P], F32, name="ident")
        make_identity(nc, ident[:])

        picked_scales = sb.tile([P, S], U8, name="picked_scales", align_bytes=64)
        nc.vector.tensor_copy(picked_scales[:], table_scales[:].indirect(offsets[:]))
        x_scale = sb.tile([P, D, V], U8, name="x_scale", align_bytes=64)
        nc.vector.tensor_copy(x_scale[:], picked_scales[:].rearrange("p (v d) -> p d v", d=D))
        x_code = sb.tile([P, D, V], U32, name="x_code", align_bytes=64)
        nc.vector.tensor_copy(
            x_code[:].rearrange("p d v -> p v d"), table_words[:].bitcast(U32).indirect(offsets[:])
        )

        def quantise(w, h, cast, codes_tag):
            name = "%s_%d" % (w, h)
            grouped = sb.tile([P, P, PACK], BF16, name="grouped_" + name, tag="grouped_" + w, align_bytes=64)
            cast(
                grouped[:].rearrange("p (c i) j -> p c j i", i=LINE),
                raw[w, h][:].rearrange("p j (c i) -> p c j i", i=LINE),
            )
            codes = sb.tile([P, P], U32, name="codes_" + name, tag=codes_tag, align_bytes=64)
            scales = sb.tile([P, P], U8, name="scales_" + name, align_bytes=64)
            nc.vector.quantize_mx(
                out=codes[:].bitcast(FP8X4), scales=scales[:], in_=grouped[:].rearrange("p n j -> p (n j)")
            )
            return codes, scales

        def product(name, quantised, planes):
            codes, scales = quantised
            y = ps.tile([P, len(planes), P], F32, name=name)
            for d in planes:
                nc.tensor.matmul_mx(
                    out=y[:, d - planes.start, :],
                    lhsT=x_code[:, d, :].bitcast(FP8X4),
                    lhsT_scale=x_scale[:, d, :],
                    rhs=codes[:].bitcast(FP8X4),
                    rhs_scale=scales[:],
                    start=True,
                    stop=True,
                )
            return y

        def sum_over_outcomes(total, terms):
            for d in range(D):
                nc.tensor.matmul(
                    total, lhsT=terms[:, d, :], rhs=ident[:], is_transpose=True, start=(d == 0), stop=(d == D - 1)
                )

        casts = (nc.scalar.copy, nc.vector.tensor_copy)
        w2_codes_tags = ("words", "codes_w2_1")
        yb_banks = ((range(0, D // 2), range(D // 2, D)), (range(D),))
        yb, yq = [], []
        for h in range(HALVES):
            w2_mx = quantise("w2", h, casts[h], w2_codes_tags[h])
            yb.append([product("yb%d_%d" % (h, planes.start), w2_mx, planes) for planes in yb_banks[h]])
            yq.append(product("yq%d" % h, quantise("w1", h, casts[h], "codes_w1_%d" % h), range(D)))

        sum_a = ps.tile([P, HALVES, V], F32, name="sum_a")
        sum_b = [ps.tile([P, V], F32, name="sum_b%d" % h) for h in range(HALVES)]
        trade_tags = ("raw_w1_0", "raw_w2_0")
        top_tags = ("raw_w1_1", "top1")
        growth_tags = ("growth0", "shifted0_0")
        parts = [slice(m0, m0 + PART) for m0 in range(0, P, PART)]
        growth, ea = [], []
        for h in range(HALVES):
            trade = sb.tile([P, D, P], F32, name="trade%d" % h, tag=trade_tags[h], align_bytes=64)
            for planes, y in zip(yb_banks[h], yb[h]):
                nc.scalar.activation(trade[:, planes.start : planes.stop, :], y[:], ACT.Tanh)
            top = sb.tile([P, P], F32, name="top%d" % h, tag=top_tags[h], align_bytes=64)
            for part in parts:
                nc.vector.tensor_reduce(top[:, part], yq[h][:, :, part].rearrange("p d m -> p m d"), AXIS.X, ALU.max)
            ea.append(sb.tile([P, D, P], F32, name="ea%d" % h))
            growth.append(sb.tile([P, D, P], F32, name="growth%d" % h, tag=growth_tags[h]))
            for planes in yb_banks[h]:
                nc.scalar.activation(
                    growth[h][:, planes.start : planes.stop, :],
                    trade[:, planes.start : planes.stop, :],
                    ACT.Exp,
                    scale=TRADE_LIMIT,
                )
            for part in parts:
                name = "shifted%d_%d" % (h, part.start)
                shifted = sb.tile([P, D, PART], F32, name=name, tag=name)
                nc.vector.tensor_tensor(
                    shifted[:],
                    yq[h][:, :, part],
                    top[:, part].unsqueeze(1).to_broadcast([P, D, PART]),
                    ALU.subtract,
                )
                nc.scalar.activation(ea[h][:, :, part], shifted[:], ACT.Exp)
        for h in range(HALVES):
            sum_over_outcomes(sum_a[:, h, :], ea[h])
            eb = sb.tile([P, D, P], F32, name="eb%d" % h)
            nc.vector.tensor_tensor(eb[:], ea[h][:], growth[h][:], ALU.mult)
            sum_over_outcomes(sum_b[h][:], eb)

        log_a = sb.tile([P, HALVES, V], F32, name="log_a")
        cost_a = sb.tile([P, HALVES, V], F32, name="cost_a")
        for h in range(HALVES):
            nc.scalar.activation(log_a[:, h, :], sum_a[:, h, :], ACT.Ln)
            nc.vector.tensor_scalar_mul(cost_a[:, h, :], log_a[:, h, :], liq_sb[:, h : h + 1])
        for h in range(HALVES):
            log_b = sb.tile([P, V], F32, name="log_b%d" % h)
            nc.scalar.activation(log_b[:], sum_b[h][:], ACT.Ln)
            result = sb.tile([P, V], F32, name="result%d" % h)
            nc.vector.scalar_tensor_tensor(
                result[:], log_b[:], liq_sb[:, h : h + 1], cost_a[:, h, :], ALU.mult, ALU.subtract
            )
            nc.sync.dma_start(out[P * h : P * (h + 1), :], result[:])
